import numpy as np
import ml_dtypes


def mxq(x, axis, fmt="e4m3"):
    dtype, down = {"e4m3": (ml_dtypes.float8_e4m3fn, 7), "e5m2": (ml_dtypes.float8_e5m2, 14)}[fmt]
    v = np.moveaxis(np.asarray(x, np.float32).astype(ml_dtypes.bfloat16).astype(np.float64), axis, -1)
    blocks = v.reshape(v.shape[:-1] + (-1, 32))
    amax = np.abs(blocks).max(-1, keepdims=True)
    byte = np.maximum(np.where(amax > 0, np.frexp(amax)[1] - 1 + 127, 0) - down, 1)
    scale = np.exp2(byte - 127.0)
    codes = (blocks / scale).astype(np.float32).astype(dtype).astype(np.float64)
    return np.moveaxis((codes * scale).reshape(v.shape), -1, axis)


WIDE = False


def mx_kscale(k):
    if not WIDE:
        return np.ones(k)
    levels = np.array([10, -10, 5, -5, 0])
    if k % 512:
        return np.exp2(np.random.permutation(np.resize(levels, k // 32))).repeat(32)
    a = np.empty((k // 512, 16))
    for p in range(k // 512):
        a[p, :8] = np.random.permutation(np.resize(levels, 8))
        for g in range(8):
            far = levels[np.abs(levels - a[p, g]) >= 10]
            a[p, g + 8] = far[np.random.randint(len(far))]
    return np.exp2(a.ravel()).repeat(32)


def f64(x):
    return np.asarray(x).astype(np.float64)


def striped(idx):
    return np.tile(idx.reshape(-1, 16).T, (8, 1)).astype(np.uint16)


def unstriped(offs):
    return offs[:16].T.reshape(-1).astype(np.int64)


def pack_weight(w):
    k, n = w.shape
    w = f64(np.asarray(w, np.float32).astype(ml_dtypes.bfloat16)).reshape(k // 32, 32, n)
    amax = np.abs(w).max(1)
    byte = np.clip(np.where(amax > 0, np.frexp(amax)[1] - 1 + 127 - 7, 1), 1, 254)
    scaled = (w * np.exp2(127.0 - byte)[:, None, :]).reshape(k, n).astype(np.float32)
    words = np.ascontiguousarray(scaled.reshape(k // 512, 128, 4, n).transpose(0, 1, 3, 2)).astype(ml_dtypes.float8_e4m3fn).view(np.uint8)
    return words, np.ascontiguousarray(byte.astype(np.uint8).reshape(k // 512, 16, n))


def unpack_weight(words, scales):
    g, p, n, _ = words.shape
    vals = np.ascontiguousarray(words).view(ml_dtypes.float8_e4m3fn).astype(np.float64) * np.repeat(np.exp2(scales.astype(np.float64) - 127.0), 8, axis=1)[..., None]
    return vals.transpose(0, 1, 3, 2).reshape(g * 512, n)


def sigmoid(v):
    return 1.0 / (1.0 + np.exp(-np.maximum(v, -700.0)))


K, T, S, D, H, Z, W = 512, 2048, 512, 2, 512, 512, 2048
P = 2 ** 7


def setup_inputs():
    n = np.random.standard_normal
    s = mx_kscale(K)[:, None]
    u = mx_kscale(H)
    packed_xT = pack_weight(n((K, T)) * s)
    packed_eT = pack_weight(n((K, W)) * s)
    return {
        "x_words": packed_xT[0],
        "x_scales": packed_xT[1],
        "w1": (n((K, H)) / np.sqrt(K) / s).astype(np.float32),
        "e_words": packed_eT[0],
        "e_scales": packed_eT[1],
        "w2": (n((K, H)) / np.sqrt(K) / s).astype(np.float32),
        "w3": (n((K, H)) / np.sqrt(K) / s).astype(np.float32),
        "unit": (np.random.uniform(0.6, 1.4, (H, 1)) * u[:, None]).astype(np.float32),
        "unit2": (np.random.uniform(0.6, 1.4, (H, 1)) / np.sqrt(H) / u[:, None]).astype(np.float32),
        "prc": (np.tile(np.random.uniform(0.1, 1.2, W), (P, 1))).astype(np.float32),
        "offs": striped(np.random.permutation(T)[:S]),
        "firm": striped(np.random.permutation(W)[:Z]),
        "ind": striped(np.random.permutation(Z)),
        "out_o": striped(np.random.permutation(Z)),
    }


def reference(x_words, x_scales, w1, e_words, e_scales, w2, w3, unit, unit2, prc, offs, firm, ind, out_o):
    xq = unpack_weight(x_words, x_scales)[:, unstriped(offs)]
    y = mxq(f64(w1), 0, "e4m3").T @ xq
    ny = -0.5 * y
    skl = np.maximum(y.reshape(len(y), -1, D).sum(axis=2), ny.reshape(len(ny), -1, D).sum(axis=2))
    hid = f64(unit) * skl
    e_firm = unpack_weight(e_words, e_scales)[:, unstriped(firm)]
    ye = mxq(f64(w2), 0, "e4m3").T @ e_firm
    yw = mxq(f64(w3), 0, "e4m3").T @ e_firm
    wi = yw[:, unstriped(ind)]
    ri = sigmoid(wi)
    fr = ye * ri
    hid2 = f64(unit2) * fr
    sc = mxq(hid, 0, "e4m3").T @ mxq(hid2, 0, "e4m3")
    net = sc - (f64(prc)[:1][:, unstriped(firm)])
    mu_ = np.exp(1.0 * np.tanh(net))
    marg = mu_.mean(axis=1, keepdims=True)
    half = mu_ / (np.sqrt(marg) + 0.2)
    return half - (0.6 * half[:, unstriped(out_o)])

import math
from contextlib import ExitStack

import concourse.mybir as mybir
from concourse.masks import make_identity

F32 = mybir.dt.float32
BF16 = mybir.dt.bfloat16
I32 = mybir.dt.int32
U32 = mybir.dt.uint32
U16 = mybir.dt.uint16
U8 = mybir.dt.uint8
FP8X4 = mybir.dt.float8_e4m3fn_x4
ALU = mybir.AluOpType
ACT = mybir.ActivationFunctionType

P = 128
PACK = 4
K = 512
H = 512
STORE = 2048
E = 512
V = 256
HALF = 256
LIST_COLS = 32

FLOPS = 2 * K * H * 512 * 3 + 2 * H * V * E
BYTES = 2 * (P * STORE * 4 + 16 * STORE) + 3 * K * H * 4 + 2 * H * 4 + STORE * 4 + 4 * P * LIST_COLS * 2 + V * E * 4


def tile_picked_ymatchm_dif_p_kernel(
    tc, x_words, x_scales, w1, e_words, e_scales, w2, w3, unit, unit2, prc, offs, firm, ind, out_o, out
):
    nc = tc.nc
    with ExitStack() as ctx:
        keep = ctx.enter_context(tc.tile_pool(name="keep", bufs=1))
        psum = ctx.enter_context(tc.psum_pool(name="psum", bufs=1))

        def sb(name, shape, dtype):
            return keep.tile(shape, dtype, name=name, align_bytes=64)

        def bank(index, shape):
            return psum.tile(shape, F32, name="bank%d" % index)

        def load_list(name, src):
            tile = sb(name, [P, LIST_COLS], U16)
            nc.sync.dma_start(tile[:], src)
            return tile

        def load_scales(name, src):
            tile = sb(name, [P, STORE], U8)
            nc.vector.memset(tile[:].bitcast(I32), 0)
            for q in range(4):
                nc.scalar.dma_start(tile[32 * q : 32 * q + 4, :].bitcast(I32), src[0, 4 * q : 4 * q + 4, :].bitcast(I32))
            return tile

        def load_words(name, src):
            tile = sb(name, [P, STORE], I32)
            nc.sync.dma_start(tile[:], src[0].rearrange("p n t -> p (n t)").bitcast(I32))
            return tile

        def load_weight(name, src):
            rows = src.rearrange("(p j) c -> p j c", j=PACK)
            halves = []
            for h in range(2):
                tile = sb("%s_raw%d" % (name, h), [P, PACK, HALF], F32)
                nc.sync.dma_start(tile[:], rows[:, :, HALF * h : HALF * (h + 1)])
                halves.append(tile)
            return halves

        def round_weight_half(copy, grouped, raw, h):
            copy(
                grouped[:, :, 64 * h : 64 * (h + 1), :].rearrange("p t m j -> p m j t"),
                raw[:].rearrange("p j (m t) -> p m j t", t=PACK),
            )

        def quantize_weight(name, grouped):
            codes = sb(name + "_codes", [P, H], U32)
            scales = sb(name + "_scales", [P, H], U8)
            for t in range(PACK):
                cols = slice(P * t, P * (t + 1))
                nc.vector.quantize_mx(codes[:, cols].bitcast(FP8X4), scales[:, cols], grouped[:, t].rearrange("p m j -> p (m j)"))
            return codes, scales

        def product(dst, lhs, lhs_cols, rhs_codes, rhs_scales, start=True, stop=True):
            nc.tensor.matmul_mx(dst, lhsT=lhs[0][:, lhs_cols].bitcast(FP8X4), lhsT_scale=lhs[1][:, lhs_cols],
                                rhs=rhs_codes.bitcast(FP8X4), rhs_scale=rhs_scales, start=start, stop=stop)

        e_scale_store = load_scales("e_scale_store", e_scales)
        w3_raw = load_weight("w3", w3)
        firm_list = load_list("firm_list", firm)
        e_word_store = load_words("e_word_store", e_words)
        x_scale_store = load_scales("x_scale_store", x_scales)
        offs_list = load_list("offs_list", offs)
        prc_store = sb("prc_store", [P, STORE], F32)
        nc.vector.memset(prc_store[:], 0.0)
        nc.scalar.dma_start(prc_store[0:1, :], prc[0:1, :])
        unit_t = sb("unit_t", [P, PACK], F32)
        unit2_t = sb("unit2_t", [P, PACK], F32)
        nc.scalar.dma_start(unit_t[:], unit.rearrange("(p t) o -> p (t o)", t=PACK))
        nc.scalar.dma_start(unit2_t[:], unit2.rearrange("(p t) o -> p (t o)", t=PACK))
        w2_raw = load_weight("w2", w2)
        ind_list = load_list("ind_list", ind)
        w1_raw = load_weight("w1", w1)
        x_word_store = load_words("x_word_store", x_words)
        out_list = load_list("out_list", out_o)

        identity = sb("identity", [P, P], F32)
        make_identity(nc, identity[:])
        one_half = sb("one_half", [P, 1], F32)
        nc.gpsimd.memset(one_half[:], 0.5)

        w3_grouped = sb("w3_grouped", [P, PACK, P, PACK], BF16)
        round_weight_half(nc.vector.tensor_copy, w3_grouped, w3_raw[0], 0)
        round_weight_half(nc.vector.tensor_copy, w3_grouped, w3_raw[1], 1)
        e_scale = sb("e_scale", [P, E], U8)
        nc.vector.tensor_copy(e_scale[:], e_scale_store[:].indirect(firm_list[:]))
        w3_q = quantize_weight("w3", w3_grouped)
        e_code = sb("e_code", [P, E], U32)
        nc.vector.tensor_copy(e_code[:], e_word_store[:].bitcast(U32).indirect(firm_list[:]))

        prc_row = sb("prc_row", [P, E], F32)
        nc.scalar.activation(prc_row[:], prc_store[:].indirect(firm_list[:]), ACT.Copy, scale=-1.0)
        prc_bank = bank(4, [P, PACK, P])
        for k in range(4):
            nc.tensor.transpose(prc_bank[:, k, :], prc_row[:, P * k : P * (k + 1)], identity[:])
        neg_prc = sb("neg_prc", [P, 4], F32)
        nc.scalar.copy(neg_prc[:], prc_bank[:, :, 0])

        unit_abs = sb("unit_abs", [P, PACK], F32)
        unit_sign = sb("unit_sign", [P, PACK], F32)
        unit2_signed = sb("unit2_signed", [P, PACK], F32)
        nc.scalar.activation(unit_abs[:], unit_t[:], ACT.Abs)
        nc.scalar.activation(unit_sign[:], unit_t[:], ACT.Sign)
        nc.gpsimd.tensor_tensor(unit2_signed[:], unit2_t[:], unit_sign[:], ALU.mult)

        x_scale = sb("x_scale", [P, 2, 2, P], U8)
        nc.vector.tensor_copy(x_scale[:].rearrange("p h d v -> p h v d"), x_scale_store[:].indirect(offs_list[:]))

        gate = []
        for t in range(PACK):
            yw = bank(t, [P, E])
            product(yw[:], w3_q, slice(P * t, P * (t + 1)), e_code[:], e_scale[:])
            g = sb("gate%d" % t, [P, E], F32)
            nc.scalar.activation(g[:], yw[:], ACT.Tanh, scale=0.5)
            gate.append(g)

        w2_grouped = sb("w2_grouped", [P, PACK, P, PACK], BF16)
        round_weight_half(nc.vector.tensor_copy, w2_grouped, w2_raw[0], 0)
        round_weight_half(nc.vector.tensor_copy, w2_grouped, w2_raw[1], 1)
        w2_q = quantize_weight("w2", w2_grouped)

        ye = []
        for h in range(2):
            cols = slice(HALF * h, HALF * (h + 1))
            for pair in range(2):
                b = bank(4 + 2 * h + pair, [P, 2, HALF])
                for u in range(2):
                    t = 2 * pair + u
                    product(b[:, u, :], w2_q, slice(P * t, P * (t + 1)), e_code[:, cols], e_scale[:, cols])
                    ye.append(b[:, u, :])

        w1_grouped = sb("w1_grouped", [P, PACK, P, PACK], BF16)

        hid2_codes = sb("hid2_codes", [P, E], U32)
        hid2_scales = sb("hid2_scales", [P, E], U8)

        def firm_half(h):
            planes = sb("hid2_planes%d" % h, [P, PACK, HALF], BF16)
            for t in range(PACK):
                ri = sb("ri%d_%d" % (h, t), [P, HALF], F32)
                nc.scalar.activation(ri[:], gate[t][:].indirect(ind_list[:, 16 * h : 16 * (h + 1)]), ACT.Copy, scale=0.5, bias=0.5)
                nc.vector.scalar_tensor_tensor(planes[:, t, :], ye[4 * h + t], unit2_signed[:, t : t + 1], ri[:], ALU.mult, ALU.mult)
            grouped = sb("hid2_grouped%d" % h, [P, HALF, PACK], BF16)
            nc.vector.tensor_copy(grouped[:].rearrange("p (c i) t -> p c t i", i=4), planes[:].rearrange("p t (c i) -> p c t i", i=4))
            cols = slice(HALF * h, HALF * (h + 1))
            nc.vector.quantize_mx(hid2_codes[:, cols].bitcast(FP8X4), hid2_scales[:, cols], grouped[:].rearrange("p e t -> p (e t)"))

        round_weight_half(nc.vector.tensor_copy, w1_grouped, w1_raw[0], 0)
        round_weight_half(nc.vector.tensor_copy, w1_grouped, w1_raw[1], 1)
        w1_q = quantize_weight("w1", w1_grouped)
        firm_half(0)

        def worker_tile(vt):
            x_code = sb("x_code%d" % vt, [P, 2, P], U32)
            nc.vector.tensor_copy(x_code[:].rearrange("p d v -> p v d"),
                                  x_word_store[:].bitcast(U32).indirect(offs_list[:, 16 * vt : 16 * (vt + 1)]))
            y = bank(vt, [P, PACK, P])
            for t in range(PACK):
                for d in range(2):
                    product(y[:, t, :], w1_q, slice(P * t, P * (t + 1)), x_code[:, d, :], x_scale[:, vt, d, :], start=(d == 0), stop=(d == 1))
            scaled = sb("scaled%d" % vt, [P, PACK, P], F32)
            for t in range(PACK):
                nc.scalar.activation(scaled[:, t, :], y[:, t, :], ACT.Copy, scale=unit_abs[:, t : t + 1])
            grouped = sb("hid_grouped%d" % vt, [P, P, PACK], BF16)
            view = scaled[:].rearrange("p t v -> p v t")
            nc.vector.scalar_tensor_tensor(grouped[:], view, -0.5, view, ALU.mult, ALU.max)
            codes = sb("hid_codes%d" % vt, [P, P], U32)
            scales = sb("hid_scales%d" % vt, [P, P], U8)
            nc.vector.quantize_mx(codes[:].bitcast(FP8X4), scales[:], grouped[:].rearrange("p v t -> p (v t)"))
            return codes, scales

        hid = [worker_tile(0)]
        firm_half(1)
        hid.append(worker_tile(1))

        def scores(vt):
            sc = bank(2 + vt, [P, 4, P])
            turned = bank(4 + vt, [P, E])
            th = sb("th%d" % vt, [P, 4, P], F32)
            for k in range(4):
                product(sc[:, k, :], (hid2_codes, hid2_scales), slice(P * k, P * (k + 1)), hid[vt][0][:], hid[vt][1][:])
            for k in range(4):
                nc.scalar.activation(th[:, k, :], sc[:, k, :], ACT.Tanh, bias=neg_prc[:, k : k + 1])
            for k in range(4):
                nc.tensor.transpose(turned[:, P * k : P * (k + 1)], th[:, k, :], identity[:])
            mu = sb("mu%d" % vt, [P, E], F32)
            total = sb("total%d" % vt, [P, 1], F32)
            nc.scalar.activation(mu[:], turned[:], ACT.Exp, accum_out=total[:])
            root = sb("root%d" % vt, [P, 1], F32)
            denom = sb("denom%d" % vt, [P, 1], F32)
            factor = sb("factor%d" % vt, [P, 1], F32)
            nc.gpsimd.tensor_tensor(root[:], total[:], one_half[:], ALU.pow)
            nc.gpsimd.tensor_scalar(denom[:], root[:], 1.0 / math.sqrt(E), 0.2, ALU.mult, ALU.add)
            nc.vector.reciprocal(factor[:], denom[:])
            return mu, factor

        def finish(vt, mu, factor):
            for h in range(2):
                cols = slice(HALF * h, HALF * (h + 1))
                offsets = out_list[:, 16 * h : 16 * (h + 1)]
                other = sb("other%d_%d" % (vt, h), [P, HALF], F32)
                if vt == 0:
                    nc.vector.tensor_copy(other[:], mu[:].indirect(offsets))
                else:
                    nc.scalar.activation(other[:], mu[:].indirect(offsets), ACT.Copy)
                diff = sb("diff%d_%d" % (vt, h), [P, HALF], F32)
                nc.vector.scalar_tensor_tensor(diff[:], other[:], -0.6, mu[:, cols], ALU.mult, ALU.add)
                res = sb("res%d_%d" % (vt, h), [P, HALF], F32)
                nc.vector.tensor_scalar(res[:], diff[:], factor[:], None, ALU.mult)
                nc.sync.dma_start(out[P * vt : P * (vt + 1), cols], res[:])

        first = scores(0)
        second = scores(1)
        finish(0, first[0], first[1])
        finish(1, second[0], second[1])
